import numpy as np
CORES = [74,78,202,206,330,334,458,462]
N = 8
def setup_inputs(rng):
    return {"x1": rng.standard_normal((N, 128, 8), dtype=np.float32), "x2": rng.standard_normal((N, 128, 128), dtype=np.float32)}
def reference(x1, x2):
    out = []
    s = x1.sum(axis=0, dtype=np.float64).astype(x1.dtype)
    out.append(np.broadcast_to(s, (N,) + s.shape))
    b = 128 // N
    bl = x2.reshape(N, 128, N, b)
    out.append(np.ascontiguousarray(bl.transpose(2, 1, 0, 3)).reshape(N, 128, 128))
    return {"y1": out[0], "y2": out[1]}

@@ -1,0 +1,120 @@
+from concourse.bass import DstId, RemoteDMATransfer
+from concourse.mybir import dt, AluOpType
+
+SCRATCH = {
+    "stage": ("sbuf", [128, 128], "float32"),
+    "land": ("sbuf", [128, 128], "float32"),
+    "dg": ("dram", [2, 128, 16], "float32"),
+    "rl": ("dram", [2, 128, 16], "float32"),
+    "dl": ("dram", [2, 128, 16], "float32"),
+    "xs": ("dram", [128, 16], "float32"),
+    "fx": ("dram", [4, 128, 16], "float32"),
+    "pb": ("dram", [128, 16], "float32"),
+    "pa": ("dram", [128, 16], "float32"),
+}
+SEMAPHORES = ["ld1", "ld2", "dirs", "dga", "dgb", "rls", "fxs", "pbs", "pas", "y1s", "acc", "st", "sent"]
+
+B = 16
+
+
+def _core(h, k):
+    return 128 * h + 72 + k
+
+
+def rank_program(g, core, T, topo):
+    if topo.chip(core) != 9:
+        return
+    h, k = topo.host(core), core % 8
+    S = T.sem
+
+    def did(dst):
+        rid, pid = topo.addr(dst, core)
+        return DstId(rid=rid, pnc=pid)
+
+    if k in (0, 4):
+        c = 0 if k == 0 else 1
+        d = (h + 1) % 4 if c == 0 else (h + 3) % 4
+        sem = S.dga if c == 0 else S.dgb
+        g.wait_ge(S.rls, 4)
+        g.remote_dma_fused([
+            RemoteDMATransfer(dst_ids=[did(_core(d, 2))], dma_engine_mask=0x0F, remote_sem=sem,
+                              src=T.rl[0], dst=T.dl[c]),
+            RemoteDMATransfer(dst_ids=[did(_core(d, 6))], dma_engine_mask=0xF0, remote_sem=sem,
+                              src=T.rl[1], dst=T.dl[c]),
+        ], local_sem=S.sent)
+        g.wait_ge(S.sent, 8)
+        return
+
+    if k == 3:
+        q = h ^ 1
+        srcs = [T.fx[i] for i in range(4)]
+        g.wait_ge(S.fxs, 16)
+        g.remote_dma_fused([
+            RemoteDMATransfer(dst_ids=[did(_core(q, 2)), did(_core(q, 6))], dma_engine_mask=0x00FF, remote_sem=S.pas,
+                              srcs=srcs, dsts=[T.pa[:], T.pa[:]], alu_op=1),
+            RemoteDMATransfer(dst_ids=[did(_core(h, 2)), did(_core(h, 6))], dma_engine_mask=0xFF00, remote_sem=S.pbs,
+                              srcs=srcs, dsts=[T.pb[:], T.pb[:]], alu_op=1),
+        ], local_sem=S.sent)
+        g.wait_ge(S.sent, 16)
+        return
+
+    if k not in (2, 6):
+        return
+
+    c = 0 if k == 2 else 1
+    r = 2 * h + c
+    d, p = (h + 2) % 4, 3 - h
+    via = (h + 1) % 4 if c == 0 else (h + 3) % 4
+    relay = _core(via, 0 if c == 0 else 4)
+
+    def blk(t, j):
+        return t[:, B * j:B * (j + 1)]
+
+    g.sync.dma_start(T.xs[0:64, :], T.x1[:]).then_inc(S.ld1, 16)
+    g.scalar.dma_start(T.xs[64:128, :], T.x1[:]).then_inc(S.ld1, 16)
+    g.scalar.dma_start(T.dg[0], blk(T.x2, 2 * d)).then_inc(S.ld1, 16)
+    g.sync.dma_start(T.dg[1], blk(T.x2, 2 * d + 1)).then_inc(S.ld1, 16)
+    g.scalar.dma_start(T.stage[:], T.x2[:]).then_inc(S.ld2, 16)
+    g.sync.dma_start(blk(T.land, r), blk(T.x2, r)).then_inc(S.dirs, 16)
+
+    g.wait_ge(S.ld1, 64)
+    g.remote_dma_fused([
+        RemoteDMATransfer(dst_ids=[did(_core(p, 3)), did(_core(h, 3))], dma_engine_mask=0xF0, remote_sem=S.fxs,
+                          srcs=[T.xs[:]], dsts=[T.fx[2 + c], T.fx[c]]),
+        RemoteDMATransfer(dst_ids=[did(relay)], dma_engine_mask=0x03, remote_sem=S.rls, src=T.dg[0], dst=T.rl[0]),
+        RemoteDMATransfer(dst_ids=[did(relay)], dma_engine_mask=0x0C, remote_sem=S.rls, src=T.dg[1], dst=T.rl[1]),
+    ], local_sem=S.sent)
+
+    g.wait_ge(S.ld2, 16)
+    trs = []
+    m = 0x03
+    for hh in ((h + 1) % 4, (h + 3) % 4):
+        for cc in (0, 1):
+            trs.append(RemoteDMATransfer(dst_ids=[did(_core(hh, 2 + 4 * cc))], dma_engine_mask=m, remote_sem=S.dirs,
+                                         src=blk(T.stage, 2 * hh + cc), dst=blk(T.land, r)))
+            m <<= 2
+    trs.append(RemoteDMATransfer(dst_ids=[did(_core(h, 6 - 4 * c))], dma_engine_mask=0xFF00, remote_sem=S.dirs,
+                                 src=blk(T.stage, 2 * h + 1 - c), dst=blk(T.land, r)))
+    g.remote_dma_fused(trs, local_sem=S.sent)
+
+    g.scalar.wait_ge(S.pbs, 8)
+    g.scalar.dma_start(T.y1[:], T.pb[0:64, :]).then_inc(S.y1s, 16)
+
+    nst = 0
+    g.sync.wait_ge(S.dirs, 16 + 8 + 8)
+    spans = {0: [(0, 64), (96, 128)], 1: [(0, 96)], 2: [(32, 128)], 3: [(0, 32), (64, 128)]}[h]
+    for lo, hi in spans:
+        g.sync.dma_start(T.y2[:, lo:hi], T.land[:, lo:hi]).then_inc(S.st, 16)
+        nst += 16
+    g.sync.wait_ge(S.dga, 4)
+    g.sync.dma_start(blk(T.y2, 2 * d), T.dl[0]).then_inc(S.st, 16)
+    g.scalar.wait_ge(S.dgb, 4)
+    g.scalar.dma_start(blk(T.y2, 2 * d + 1), T.dl[1]).then_inc(S.st, 16)
+    nst += 32
+
+    g.wait_ge(S.y1s, 16)
+    g.wait_ge(S.pas, 8)
+    g.dma_start(T.y1[:], T.pa[0:64, :], accum_op=AluOpType.add).then_inc(S.acc, 16)
+    g.wait_ge(S.sent, 8 + 16)
+    g.wait_ge(S.st, nst)
+    g.wait_ge(S.acc, 16)

@@ -1,18 +1,22 @@
 from concourse.bass import DstId, RemoteDMATransfer
 from concourse.mybir import dt, AluOpType
 
+AR = "first"
+FIN = "accum"
+W = 16 if AR == "fused" else 8
+
 SCRATCH = {
     "stage": ("sbuf", [128, 128], "float32"),
     "land": ("sbuf", [128, 128], "float32"),
     "dg": ("dram", [2, 128, 16], "float32"),
     "rl": ("dram", [2, 128, 16], "float32"),
     "dl": ("dram", [2, 128, 16], "float32"),
-    "xs": ("dram", [128, 16], "float32"),
-    "fx": ("dram", [4, 128, 16], "float32"),
-    "pb": ("dram", [128, 16], "float32"),
-    "pa": ("dram", [128, 16], "float32"),
+    "xs": ("dram", [128, W], "float32"),
+    "fx": ("dram", [4, 128, W], "float32"),
+    "pb": ("dram", [128, W], "float32"),
+    "pa": ("dram", [128, W], "float32"),
 }
-SEMAPHORES = ["ld1", "ld2", "dirs", "dga", "dgb", "rls", "fxs", "pbs", "pas", "y1s", "acc", "st", "sent"]
+SEMAPHORES = ["ld0", "ld1", "ld2", "dirs", "dga", "dgb", "rls", "fxs", "pbs", "pas", "y1s", "acc", "st", "sent"]
 
 B = 16
 
@@ -35,7 +39,7 @@ def rank_program(g, core, T, topo):
         c = 0 if k == 0 else 1
         d = (h + 1) % 4 if c == 0 else (h + 3) % 4
         sem = S.dga if c == 0 else S.dgb
-        g.wait_ge(S.rls, 4)
+        g.wait_ge(S.rls, 8 if AR != "fused" else 4)
         g.remote_dma_fused([
             RemoteDMATransfer(dst_ids=[did(_core(d, 2))], dma_engine_mask=0x0F, remote_sem=sem,
                               src=T.rl[0], dst=T.dl[c]),
@@ -48,14 +52,26 @@ def rank_program(g, core, T, topo):
     if k == 3:
         q = h ^ 1
         srcs = [T.fx[i] for i in range(4)]
-        g.wait_ge(S.fxs, 16)
-        g.remote_dma_fused([
-            RemoteDMATransfer(dst_ids=[did(_core(q, 2)), did(_core(q, 6))], dma_engine_mask=0x00FF, remote_sem=S.pas,
-                              srcs=srcs, dsts=[T.pa[:], T.pa[:]], alu_op=1),
-            RemoteDMATransfer(dst_ids=[did(_core(h, 2)), did(_core(h, 6))], dma_engine_mask=0xFF00, remote_sem=S.pbs,
-                              srcs=srcs, dsts=[T.pb[:], T.pb[:]], alu_op=1),
-        ], local_sem=S.sent)
-        g.wait_ge(S.sent, 16)
+        g.wait_ge(S.fxs, 4 * (4 if AR == "fused" else 8))
+        if FIN == "accum":
+            g.remote_dma_fused([
+                RemoteDMATransfer(dst_ids=[did(_core(q, 2)), did(_core(q, 6))], dma_engine_mask=0x00FF,
+                                  remote_sem=S.pas, srcs=srcs, dsts=[T.pa[:], T.pa[:]], alu_op=1),
+                RemoteDMATransfer(dst_ids=[did(_core(h, 2)), did(_core(h, 6))], dma_engine_mask=0xFF00,
+                                  remote_sem=S.pbs, srcs=srcs, dsts=[T.pb[:], T.pb[:]], alu_op=1),
+            ], local_sem=S.sent)
+            g.wait_ge(S.sent, 16)
+        else:
+            g.remote_dma_fused([
+                RemoteDMATransfer(dst_ids=[did(_core(q, 3))], dma_engine_mask=0x00FF,
+                                  remote_sem=S.pas, srcs=srcs, dsts=[T.pa[:]], alu_op=1),
+            ], local_sem=S.sent)
+            g.wait_ge(S.pas, 8)
+            g.remote_dma_fused([
+                RemoteDMATransfer(dst_ids=[did(_core(h, 2)), did(_core(h, 6))], dma_engine_mask=0xFFFF,
+                                  remote_sem=S.pbs, srcs=srcs + [T.pa[:]], dsts=[T.pb[:], T.pb[:]], alu_op=1),
+            ], local_sem=S.sent)
+            g.wait_ge(S.sent, 24)
         return
 
     if k not in (2, 6):
@@ -66,24 +82,42 @@ def rank_program(g, core, T, topo):
     d, p = (h + 2) % 4, 3 - h
     via = (h + 1) % 4 if c == 0 else (h + 3) % 4
     relay = _core(via, 0 if c == 0 else 4)
+    nsent = 0
 
     def blk(t, j):
         return t[:, B * j:B * (j + 1)]
 
-    g.sync.dma_start(T.xs[0:64, :], T.x1[:]).then_inc(S.ld1, 16)
-    g.scalar.dma_start(T.xs[64:128, :], T.x1[:]).then_inc(S.ld1, 16)
+    def x1_transfer(mask):
+        return RemoteDMATransfer(dst_ids=[did(_core(p, 3)), did(_core(h, 3))], dma_engine_mask=mask, remote_sem=S.fxs,
+                                 srcs=[T.xs[:]], dsts=[T.fx[2 + c], T.fx[c]])
+
+    if AR == "fused":
+        g.sync.dma_start(T.xs[0:64, :], T.x1[:]).then_inc(S.ld1, 16)
+        g.scalar.dma_start(T.xs[64:128, :], T.x1[:]).then_inc(S.ld1, 16)
+        nld1 = 64
+    else:
+        g.sync.dma_start(T.xs[:], T.x1[:]).then_inc(S.ld0, 16)
+        nld1 = 32
     g.scalar.dma_start(T.dg[0], blk(T.x2, 2 * d)).then_inc(S.ld1, 16)
     g.sync.dma_start(T.dg[1], blk(T.x2, 2 * d + 1)).then_inc(S.ld1, 16)
     g.scalar.dma_start(T.stage[:], T.x2[:]).then_inc(S.ld2, 16)
     g.sync.dma_start(blk(T.land, r), blk(T.x2, r)).then_inc(S.dirs, 16)
 
-    g.wait_ge(S.ld1, 64)
-    g.remote_dma_fused([
-        RemoteDMATransfer(dst_ids=[did(_core(p, 3)), did(_core(h, 3))], dma_engine_mask=0xF0, remote_sem=S.fxs,
-                          srcs=[T.xs[:]], dsts=[T.fx[2 + c], T.fx[c]]),
-        RemoteDMATransfer(dst_ids=[did(relay)], dma_engine_mask=0x03, remote_sem=S.rls, src=T.dg[0], dst=T.rl[0]),
-        RemoteDMATransfer(dst_ids=[did(relay)], dma_engine_mask=0x0C, remote_sem=S.rls, src=T.dg[1], dst=T.rl[1]),
-    ], local_sem=S.sent)
+    if AR == "first":
+        g.wait_ge(S.ld0, 16)
+        g.remote_dma_fused([x1_transfer(0xFF)], local_sem=S.sent)
+        nsent += 8
+
+    g.wait_ge(S.ld1, nld1)
+    if AR == "fused":
+        trs = [x1_transfer(0xF0),
+               RemoteDMATransfer(dst_ids=[did(relay)], dma_engine_mask=0x03, remote_sem=S.rls, src=T.dg[0], dst=T.rl[0]),
+               RemoteDMATransfer(dst_ids=[did(relay)], dma_engine_mask=0x0C, remote_sem=S.rls, src=T.dg[1], dst=T.rl[1])]
+    else:
+        trs = [RemoteDMATransfer(dst_ids=[did(relay)], dma_engine_mask=0x0F, remote_sem=S.rls, src=T.dg[0], dst=T.rl[0]),
+               RemoteDMATransfer(dst_ids=[did(relay)], dma_engine_mask=0xF0, remote_sem=S.rls, src=T.dg[1], dst=T.rl[1])]
+    g.remote_dma_fused(trs, local_sem=S.sent)
+    nsent += 8
 
     g.wait_ge(S.ld2, 16)
     trs = []
@@ -96,9 +130,18 @@ def rank_program(g, core, T, topo):
     trs.append(RemoteDMATransfer(dst_ids=[did(_core(h, 6 - 4 * c))], dma_engine_mask=0xFF00, remote_sem=S.dirs,
                                  src=blk(T.stage, 2 * h + 1 - c), dst=blk(T.land, r)))
     g.remote_dma_fused(trs, local_sem=S.sent)
+    nsent += 16
 
-    g.scalar.wait_ge(S.pbs, 8)
-    g.scalar.dma_start(T.y1[:], T.pb[0:64, :]).then_inc(S.y1s, 16)
+    if AR == "last":
+        g.wait_ge(S.ld0, 16)
+        g.remote_dma_fused([x1_transfer(0xFF)], local_sem=S.sent)
+        nsent += 8
+
+    pb = T.pb[0:64, :] if AR == "fused" else T.pb[:]
+    pa = T.pa[0:64, :] if AR == "fused" else T.pa[:]
+
+    g.scalar.wait_ge(S.pbs, 8 if FIN == "accum" else 16)
+    g.scalar.dma_start(T.y1[:], pb).then_inc(S.y1s, 16)
 
     nst = 0
     g.sync.wait_ge(S.dirs, 16 + 8 + 8)
@@ -113,8 +156,10 @@ def rank_program(g, core, T, topo):
     nst += 32
 
     g.wait_ge(S.y1s, 16)
-    g.wait_ge(S.pas, 8)
-    g.dma_start(T.y1[:], T.pa[0:64, :], accum_op=AluOpType.add).then_inc(S.acc, 16)
-    g.wait_ge(S.sent, 8 + 16)
+    if FIN == "accum":
+        g.wait_ge(S.pas, 8)
+        g.dma_start(T.y1[:], pa, accum_op=AluOpType.add).then_inc(S.acc, 16)
+    g.wait_ge(S.sent, nsent)
     g.wait_ge(S.st, nst)
-    g.wait_ge(S.acc, 16)
+    if FIN == "accum":
+        g.wait_ge(S.acc, 16)

@@ -1,20 +1,16 @@
 from concourse.bass import DstId, RemoteDMATransfer
 from concourse.mybir import dt, AluOpType
 
-AR = "first"
-FIN = "accum"
-W = 16 if AR == "fused" else 8
-
 SCRATCH = {
     "stage": ("sbuf", [128, 128], "float32"),
     "land": ("sbuf", [128, 128], "float32"),
     "dg": ("dram", [2, 128, 16], "float32"),
     "rl": ("dram", [2, 128, 16], "float32"),
     "dl": ("dram", [2, 128, 16], "float32"),
-    "xs": ("dram", [128, W], "float32"),
-    "fx": ("dram", [4, 128, W], "float32"),
-    "pb": ("dram", [128, W], "float32"),
-    "pa": ("dram", [128, W], "float32"),
+    "xs": ("dram", [128, 8], "float32"),
+    "fx": ("dram", [4, 128, 8], "float32"),
+    "pb": ("dram", [128, 8], "float32"),
+    "pa": ("dram", [128, 8], "float32"),
 }
 SEMAPHORES = ["ld0", "ld1", "ld2", "dirs", "dga", "dgb", "rls", "fxs", "pbs", "pas", "y1s", "acc", "st", "sent"]
 
@@ -30,48 +26,33 @@ def rank_program(g, core, T, topo):
         return
     h, k = topo.host(core), core % 8
     S = T.sem
+    p, q = 3 - h, h ^ 1
 
     def did(dst):
         rid, pid = topo.addr(dst, core)
         return DstId(rid=rid, pnc=pid)
 
+    def tr(dsts, mask, sem, srcs, outs, op=0):
+        return RemoteDMATransfer(dst_ids=[did(x) for x in dsts], dma_engine_mask=mask, remote_sem=sem,
+                                 srcs=srcs, dsts=outs, alu_op=op)
+
     if k in (0, 4):
         c = 0 if k == 0 else 1
         d = (h + 1) % 4 if c == 0 else (h + 3) % 4
         sem = S.dga if c == 0 else S.dgb
-        g.wait_ge(S.rls, 8 if AR != "fused" else 4)
-        g.remote_dma_fused([
-            RemoteDMATransfer(dst_ids=[did(_core(d, 2))], dma_engine_mask=0x0F, remote_sem=sem,
-                              src=T.rl[0], dst=T.dl[c]),
-            RemoteDMATransfer(dst_ids=[did(_core(d, 6))], dma_engine_mask=0xF0, remote_sem=sem,
-                              src=T.rl[1], dst=T.dl[c]),
-        ], local_sem=S.sent)
+        g.wait_ge(S.rls, 8)
+        g.remote_dma_fused([tr([_core(d, 2)], 0x0F, sem, [T.rl[0]], [T.dl[c]]),
+                            tr([_core(d, 6)], 0xF0, sem, [T.rl[1]], [T.dl[c]])], local_sem=S.sent)
         g.wait_ge(S.sent, 8)
         return
 
     if k == 3:
-        q = h ^ 1
         srcs = [T.fx[i] for i in range(4)]
-        g.wait_ge(S.fxs, 4 * (4 if AR == "fused" else 8))
-        if FIN == "accum":
-            g.remote_dma_fused([
-                RemoteDMATransfer(dst_ids=[did(_core(q, 2)), did(_core(q, 6))], dma_engine_mask=0x00FF,
-                                  remote_sem=S.pas, srcs=srcs, dsts=[T.pa[:], T.pa[:]], alu_op=1),
-                RemoteDMATransfer(dst_ids=[did(_core(h, 2)), did(_core(h, 6))], dma_engine_mask=0xFF00,
-                                  remote_sem=S.pbs, srcs=srcs, dsts=[T.pb[:], T.pb[:]], alu_op=1),
-            ], local_sem=S.sent)
-            g.wait_ge(S.sent, 16)
-        else:
-            g.remote_dma_fused([
-                RemoteDMATransfer(dst_ids=[did(_core(q, 3))], dma_engine_mask=0x00FF,
-                                  remote_sem=S.pas, srcs=srcs, dsts=[T.pa[:]], alu_op=1),
-            ], local_sem=S.sent)
-            g.wait_ge(S.pas, 8)
-            g.remote_dma_fused([
-                RemoteDMATransfer(dst_ids=[did(_core(h, 2)), did(_core(h, 6))], dma_engine_mask=0xFFFF,
-                                  remote_sem=S.pbs, srcs=srcs + [T.pa[:]], dsts=[T.pb[:], T.pb[:]], alu_op=1),
-            ], local_sem=S.sent)
-            g.wait_ge(S.sent, 24)
+        g.wait_ge(S.fxs, 32)
+        g.remote_dma_fused([tr([_core(q, 2), _core(q, 6)], 0x00FF, S.pas, srcs, [T.pa[:], T.pa[:]], 1),
+                            tr([_core(h, 2), _core(h, 6)], 0xFF00, S.pbs, srcs, [T.pb[:], T.pb[:]], 1)],
+                           local_sem=S.sent)
+        g.wait_ge(S.sent, 16)
         return
 
     if k not in (2, 6):
@@ -79,69 +60,38 @@ def rank_program(g, core, T, topo):
 
     c = 0 if k == 2 else 1
     r = 2 * h + c
-    d, p = (h + 2) % 4, 3 - h
+    d = (h + 2) % 4
     via = (h + 1) % 4 if c == 0 else (h + 3) % 4
     relay = _core(via, 0 if c == 0 else 4)
-    nsent = 0
 
     def blk(t, j):
         return t[:, B * j:B * (j + 1)]
 
-    def x1_transfer(mask):
-        return RemoteDMATransfer(dst_ids=[did(_core(p, 3)), did(_core(h, 3))], dma_engine_mask=mask, remote_sem=S.fxs,
-                                 srcs=[T.xs[:]], dsts=[T.fx[2 + c], T.fx[c]])
-
-    if AR == "fused":
-        g.sync.dma_start(T.xs[0:64, :], T.x1[:]).then_inc(S.ld1, 16)
-        g.scalar.dma_start(T.xs[64:128, :], T.x1[:]).then_inc(S.ld1, 16)
-        nld1 = 64
-    else:
-        g.sync.dma_start(T.xs[:], T.x1[:]).then_inc(S.ld0, 16)
-        nld1 = 32
+    g.sync.dma_start(T.xs[:], T.x1[:]).then_inc(S.ld0, 16)
     g.scalar.dma_start(T.dg[0], blk(T.x2, 2 * d)).then_inc(S.ld1, 16)
     g.sync.dma_start(T.dg[1], blk(T.x2, 2 * d + 1)).then_inc(S.ld1, 16)
     g.scalar.dma_start(T.stage[:], T.x2[:]).then_inc(S.ld2, 16)
     g.sync.dma_start(blk(T.land, r), blk(T.x2, r)).then_inc(S.dirs, 16)
 
-    if AR == "first":
-        g.wait_ge(S.ld0, 16)
-        g.remote_dma_fused([x1_transfer(0xFF)], local_sem=S.sent)
-        nsent += 8
+    g.wait_ge(S.ld0, 16)
+    g.remote_dma_fused([tr([_core(p, 3), _core(h, 3)], 0xFF, S.fxs, [T.xs[:]], [T.fx[2 + c], T.fx[c]])], local_sem=S.sent)
 
-    g.wait_ge(S.ld1, nld1)
-    if AR == "fused":
-        trs = [x1_transfer(0xF0),
-               RemoteDMATransfer(dst_ids=[did(relay)], dma_engine_mask=0x03, remote_sem=S.rls, src=T.dg[0], dst=T.rl[0]),
-               RemoteDMATransfer(dst_ids=[did(relay)], dma_engine_mask=0x0C, remote_sem=S.rls, src=T.dg[1], dst=T.rl[1])]
-    else:
-        trs = [RemoteDMATransfer(dst_ids=[did(relay)], dma_engine_mask=0x0F, remote_sem=S.rls, src=T.dg[0], dst=T.rl[0]),
-               RemoteDMATransfer(dst_ids=[did(relay)], dma_engine_mask=0xF0, remote_sem=S.rls, src=T.dg[1], dst=T.rl[1])]
-    g.remote_dma_fused(trs, local_sem=S.sent)
-    nsent += 8
+    g.wait_ge(S.ld1, 32)
+    g.remote_dma_fused([tr([relay], 0x0F, S.rls, [T.dg[0]], [T.rl[0]]),
+                        tr([relay], 0xF0, S.rls, [T.dg[1]], [T.rl[1]])], local_sem=S.sent)
 
     g.wait_ge(S.ld2, 16)
     trs = []
     m = 0x03
     for hh in ((h + 1) % 4, (h + 3) % 4):
         for cc in (0, 1):
-            trs.append(RemoteDMATransfer(dst_ids=[did(_core(hh, 2 + 4 * cc))], dma_engine_mask=m, remote_sem=S.dirs,
-                                         src=blk(T.stage, 2 * hh + cc), dst=blk(T.land, r)))
+            trs.append(tr([_core(hh, 2 + 4 * cc)], m, S.dirs, [blk(T.stage, 2 * hh + cc)], [blk(T.land, r)]))
             m <<= 2
-    trs.append(RemoteDMATransfer(dst_ids=[did(_core(h, 6 - 4 * c))], dma_engine_mask=0xFF00, remote_sem=S.dirs,
-                                 src=blk(T.stage, 2 * h + 1 - c), dst=blk(T.land, r)))
+    trs.append(tr([_core(h, 6 - 4 * c)], 0xFF00, S.dirs, [blk(T.stage, 2 * h + 1 - c)], [blk(T.land, r)]))
     g.remote_dma_fused(trs, local_sem=S.sent)
-    nsent += 16
 
-    if AR == "last":
-        g.wait_ge(S.ld0, 16)
-        g.remote_dma_fused([x1_transfer(0xFF)], local_sem=S.sent)
-        nsent += 8
-
-    pb = T.pb[0:64, :] if AR == "fused" else T.pb[:]
-    pa = T.pa[0:64, :] if AR == "fused" else T.pa[:]
-
-    g.scalar.wait_ge(S.pbs, 8 if FIN == "accum" else 16)
-    g.scalar.dma_start(T.y1[:], pb).then_inc(S.y1s, 16)
+    g.scalar.wait_ge(S.pbs, 8)
+    g.scalar.dma_start(T.y1[:], T.pb[:]).then_inc(S.y1s, 16)
 
     nst = 0
     g.sync.wait_ge(S.dirs, 16 + 8 + 8)
@@ -156,10 +106,8 @@ def rank_program(g, core, T, topo):
     nst += 32
 
     g.wait_ge(S.y1s, 16)
-    if FIN == "accum":
-        g.wait_ge(S.pas, 8)
-        g.dma_start(T.y1[:], pa, accum_op=AluOpType.add).then_inc(S.acc, 16)
-    g.wait_ge(S.sent, nsent)
+    g.wait_ge(S.pas, 8)
+    g.dma_start(T.y1[:], T.pa[:], accum_op=AluOpType.add).then_inc(S.acc, 16)
+    g.wait_ge(S.sent, 8 + 8 + 16)
     g.wait_ge(S.st, nst)
-    if FIN == "accum":
-        g.wait_ge(S.acc, 16)
+    g.wait_ge(S.acc, 16)

from concourse.bass import DstId, RemoteDMATransfer
from concourse.mybir import dt, AluOpType

SCRATCH = {
    "stage": ("sbuf", [128, 128], "float32"),
    "land": ("sbuf", [128, 128], "float32"),
    "dg": ("dram", [2, 128, 16], "float32"),
    "rl": ("dram", [2, 128, 16], "float32"),
    "dl": ("dram", [2, 128, 16], "float32"),
    "xs": ("dram", [128, 8], "float32"),
    "fx": ("dram", [4, 128, 8], "float32"),
    "pb": ("dram", [128, 8], "float32"),
    "pa": ("dram", [128, 8], "float32"),
}
SEMAPHORES = ["ld0", "ld1", "ld2", "dirs", "dga", "dgb", "rls", "fxs", "pbs", "pas", "y1s", "acc", "st", "sent"]

B = 16


def _core(h, k):
    return 128 * h + 72 + k


def rank_program(g, core, T, topo):
    if topo.chip(core) != 9:
        return
    h, k = topo.host(core), core % 8
    S = T.sem
    p, q = 3 - h, h ^ 1

    def did(dst):
        rid, pid = topo.addr(dst, core)
        return DstId(rid=rid, pnc=pid)

    def tr(dsts, mask, sem, srcs, outs, op=0):
        return RemoteDMATransfer(dst_ids=[did(x) for x in dsts], dma_engine_mask=mask, remote_sem=sem,
                                 srcs=srcs, dsts=outs, alu_op=op)

    if k in (0, 4):
        c = 0 if k == 0 else 1
        d = (h + 1) % 4 if c == 0 else (h + 3) % 4
        sem = S.dga if c == 0 else S.dgb
        g.wait_ge(S.rls, 8)
        g.remote_dma_fused([tr([_core(d, 2)], 0x0F, sem, [T.rl[0]], [T.dl[c]]),
                            tr([_core(d, 6)], 0xF0, sem, [T.rl[1]], [T.dl[c]])], local_sem=S.sent)
        g.wait_ge(S.sent, 8)
        return

    if k == 3:
        srcs = [T.fx[i] for i in range(4)]
        g.wait_ge(S.fxs, 32)
        g.remote_dma_fused([tr([_core(q, 2), _core(q, 6)], 0x00FF, S.pas, srcs, [T.pa[:], T.pa[:]], 1),
                            tr([_core(h, 2), _core(h, 6)], 0xFF00, S.pbs, srcs, [T.pb[:], T.pb[:]], 1)],
                           local_sem=S.sent)
        g.wait_ge(S.sent, 16)
        return

    if k not in (2, 6):
        return

    c = 0 if k == 2 else 1
    r = 2 * h + c
    d = (h + 2) % 4
    via = (h + 1) % 4 if c == 0 else (h + 3) % 4
    relay = _core(via, 0 if c == 0 else 4)

    def blk(t, j):
        return t[:, B * j:B * (j + 1)]

    g.sync.dma_start(T.xs[:], T.x1[:]).then_inc(S.ld0, 16)
    g.scalar.dma_start(T.dg[0], blk(T.x2, 2 * d)).then_inc(S.ld1, 16)
    g.sync.dma_start(T.dg[1], blk(T.x2, 2 * d + 1)).then_inc(S.ld1, 16)
    g.scalar.dma_start(T.stage[:], T.x2[:]).then_inc(S.ld2, 16)
    g.sync.dma_start(blk(T.land, r), blk(T.x2, r)).then_inc(S.dirs, 16)

    g.wait_ge(S.ld0, 16)
    g.remote_dma_fused([tr([_core(p, 3), _core(h, 3)], 0xFF, S.fxs, [T.xs[:]], [T.fx[2 + c], T.fx[c]])], local_sem=S.sent)

    g.wait_ge(S.ld1, 32)
    g.remote_dma_fused([tr([relay], 0x0F, S.rls, [T.dg[0]], [T.rl[0]]),
                        tr([relay], 0xF0, S.rls, [T.dg[1]], [T.rl[1]])], local_sem=S.sent)

    g.wait_ge(S.ld2, 16)
    trs = []
    m = 0x03
    for hh in ((h + 1) % 4, (h + 3) % 4):
        for cc in (0, 1):
            trs.append(tr([_core(hh, 2 + 4 * cc)], m, S.dirs, [blk(T.stage, 2 * hh + cc)], [blk(T.land, r)]))
            m <<= 2
    trs.append(tr([_core(h, 6 - 4 * c)], 0xFF00, S.dirs, [blk(T.stage, 2 * h + 1 - c)], [blk(T.land, r)]))
    g.remote_dma_fused(trs, local_sem=S.sent)

    g.scalar.wait_ge(S.pbs, 8)
    g.scalar.dma_start(T.y1[:], T.pb[:]).then_inc(S.y1s, 16)

    nst = 0
    g.sync.wait_ge(S.dirs, 16 + 8 + 8)
    spans = {0: [(0, 64), (96, 128)], 1: [(0, 96)], 2: [(32, 128)], 3: [(0, 32), (64, 128)]}[h]
    for lo, hi in spans:
        g.sync.dma_start(T.y2[:, lo:hi], T.land[:, lo:hi]).then_inc(S.st, 16)
        nst += 16
    g.sync.wait_ge(S.dga, 4)
    g.sync.dma_start(blk(T.y2, 2 * d), T.dl[0]).then_inc(S.st, 16)
    g.scalar.wait_ge(S.dgb, 4)
    g.scalar.dma_start(blk(T.y2, 2 * d + 1), T.dl[1]).then_inc(S.st, 16)
    nst += 32

    g.wait_ge(S.y1s, 16)
    g.wait_ge(S.pas, 8)
    g.dma_start(T.y1[:], T.pa[:], accum_op=AluOpType.add).then_inc(S.acc, 16)
    g.wait_ge(S.sent, 8 + 8 + 16)
    g.wait_ge(S.st, nst)
    g.wait_ge(S.acc, 16)
